import numpy as np, ml_dtypes
CORES = [5,29,101,125,133,157,229,253]
N = 8
import mx_ref
BF = ml_dtypes.bfloat16
def gentries(a):
    return np.ascontiguousarray(a.reshape(8, 16, -1).transpose(0, 2, 1)).reshape(8, -1)
def gtable(e):
    e = np.asarray(e); return np.ascontiguousarray(e.reshape(8, -1, 16).transpose(0, 2, 1)).reshape(128, -1).astype(np.int32)
def gcols(t, e):
    v = np.concatenate([t.reshape(8, 16, -1, 4), np.zeros((8, 16, 1, 4), BF)], axis=2)
    return np.ascontiguousarray(np.stack([v[g][:, e[g]] for g in range(8)])).reshape(128, -1)
def f(rng, *shape):
    return mx_ref.flush((rng.standard_normal(shape, dtype=np.float32) * np.exp2(rng.integers(-2, 3, shape[:-1] + (1,)))).astype(BF))
def wide(rng, *shape, cols=0):
    v = rng.standard_normal(shape, dtype=np.float32) * np.exp2(rng.integers(-12, 13, shape)).astype(np.float32)
    if cols: v *= np.repeat(np.exp2(rng.integers(-cols, cols + 1, shape[:-2] + (1, shape[-1] // 4))) * (rng.random(shape[:-2] + (1, shape[-1] // 4)) > 0.0625), 4, axis=-1).astype(np.float32)
    return mx_ref.flush(v.astype(BF))
S = 128
def block(rng, how):
    if how == "one": return np.full((8, S), rng.integers(0, 128))
    if how == "groups": return np.tile(rng.integers(0, 128, S), (8, 1))
    if how == "ends": return np.stack([rng.permutation(np.arange(S) % 2 * 127) for g in range(8)])
    if how == "distinct": return np.stack([np.tile(rng.permutation(128), S // 128) for g in range(8)])
    return rng.integers(0, 128, (8, S))
def lists(rng, how=""):
    return {"cw": np.stack([gtable(np.concatenate([block(rng, how) for s in range(N)], axis=1)) for r in range(N)])}
def setup_inputs(rng):
    return {"bk": f(rng, N, 128, 512), "x": f(rng, N, 128, 512 * N), **lists(rng)}
def setup_inputs_one(rng):
    return {**setup_inputs(rng), **lists(rng, "one")}
def setup_inputs_groups(rng):
    return {**setup_inputs(rng), **lists(rng, "groups")}
def setup_inputs_ends(rng):
    return {**setup_inputs(rng), **lists(rng, "ends")}
def setup_inputs_distinct(rng):
    return {**setup_inputs(rng), **lists(rng, "distinct")}
def setup_inputs_spread(rng):
    d = setup_inputs(rng); d["bk"] = wide(rng, N, 128, 512, cols=4); d["x"] = wide(rng, N, 128, 512 * N); return d
def check_inputs(d):
    b = []
    for r in range(N):
        e = d["cw"][r]
        if e.min() < 0 or e.max() > 127: b.append("cw")
    return b
def reference(bk, x, cw):
    y = np.zeros((N, 128, S), np.float32)
    for r in range(N):
        e = gentries(cw[r])
        for s in range(N):
            W = gcols(bk[s], e[:, S * s:S * s + S])
            X = np.ascontiguousarray(x[r][:, 512 * s:512 * s + 512])
            y[r] += mx_ref.matmul(mx_ref.quantize(X), mx_ref.quantize(W))
    return {"y": y}

@@ -1,0 +1,218 @@
+from concourse.bass import DstId, RemoteDMATransfer
+from concourse.mybir import dt, ActivationFunctionType
+
+N = 8
+S = 128
+K = S // 16
+SCRATCH = {
+    "lst": ("sbuf", [128, N * K], "int32"),
+    "l16": ("sbuf", [128, N * K], "uint16"),
+    "book": ("sbuf", [128, 4 * S], "bfloat16"),
+    "win": ("sbuf", [128, 4 * S], "bfloat16"),
+    "offd": ("sbuf", [128, 3 * K], "uint16"),
+    "offo": ("sbuf", [128, 4 * K], "uint16"),
+    "h": ("sbuf", [128, 4 * S * N], "bfloat16"),
+    "qc": ("sbuf", [128, S * N], "float8_e4m3fn_x4"),
+    "qs": ("sbuf", [128, S * N], "uint8"),
+    "xt": ("sbuf", [128, 4 * S * N], "bfloat16"),
+    "xc": ("sbuf", [128, S * N], "float8_e4m3fn_x4"),
+    "xs": ("sbuf", [128, S * N], "uint8"),
+    "wc": ("sbuf", [128, S * N], "float8_e4m3fn_x4"),
+    "ws": ("sbuf", [128, S * N], "uint8"),
+    "ps": ("psum", [128, 512], "float32"),
+    "yt": ("sbuf", [128, S], "float32"),
+    "rlist": ("sbuf", [128, K], "uint16"),
+    "rcode": ("sbuf", [128, S], "float8_e4m3fn_x4"),
+    "rscal": ("sbuf", [128, S], "uint8"),
+}
+SEMAPHORES = (["cwl", "bkl", "x0", "x1", "conv", "vd", "sd", "lsent", "tsent", "ld", "lo0", "lo1", "qx0", "qx1", "mm", "ev",
+               "st", "rl", "rc", "rs", "rsent"]
+              + ["gv%d" % i for i in range(4)] + ["gs%d" % i for i in range(4)] + ["q%d" % i for i in range(4)]
+              + ["t%d" % i for i in range(N)])
+
+
+def bits(engines):
+    m = 0
+    for e in engines:
+        m |= 1 << e
+    return m
+
+
+def plan(T, topo, rank):
+    me = T.cores[rank]
+    direct = [r for r in range(N) if r != rank and topo.may_write(me, T.cores[r])]
+    cross = [r for r in range(N) if r != rank and r not in direct]
+    a = sorted(direct + [rank]).index(rank) % len(cross)
+    cross = cross[a:] + cross[:a]
+    cand = [c for c in topo.cores_of(me) if c != me and all(topo.may_write(c, T.cores[r]) for r in cross)]
+    near = [c for c in cand if topo.die(c) == topo.die(me)]
+    far = [c for c in cand if topo.die(c) != topo.die(me)]
+    relays = []
+    for i in range(max(len(near), len(far))):
+        relays += far[i:i + 1] + near[i:i + 1]
+    return direct, cross, relays[:len(cross)]
+
+
+def rank_program(g, core, T, topo):
+    rank = T.rank_of(core)
+    if rank is None:
+        relay_program(g, core, T, topo)
+        return
+    sem = T.sem
+    direct, cross, relays = plan(T, topo, rank)
+    copy = ActivationFunctionType.Copy
+    off = topo.engines(core, T.cores[direct[0]])
+    spare = [e for e in topo.engines(core, relays[0]) if e not in off]
+
+    def transfer(to, engines, rsem, src, dst):
+        rid, pid = topo.addr(to, core)
+        return RemoteDMATransfer(dst_ids=[DstId(rid=rid, pnc=pid)], dma_engine_mask=bits(engines), remote_sem=rsem,
+                                 src=src, dst=dst)
+
+    eg_list = [spare[2 * i:2 * i + 2] for i in range(4)]
+    eg_dir = [off[0:2], off[2:4], off[4:8]]
+    eg_half = [[spare[0:4], spare[4:8]], [off[0:4] + spare[0:4], off[4:8] + spare[4:8]]]
+
+    g.sync.dma_start(T.lst[:], T.cw[:]).then_inc(sem.cwl, 16)
+    g.sync.dma_start(T.book[:], T.bk[:]).then_inc(sem.bkl, 16)
+    nlist = sum(len(e) for e in eg_list) + sum(len(e) for e in eg_dir)
+    g.sync.wait_ge(sem.lsent, nlist)
+    half = 2 * S * N
+    for i in range(2):
+        g.sync.dma_start(T.xt[:, i * half:(i + 1) * half], T.x[:, i * half:(i + 1) * half]).then_inc(sem["x%d" % i], 16)
+
+    g.wait_ge(sem.conv, 1)
+    tr = []
+    for i in range(4):
+        d = cross[i]
+        tr.append(transfer(relays[i], eg_list[i], sem.rl, T.l16[:, K * d:K * d + K], T.rlist[:]))
+    g.remote_dma_fused(tr, local_sem=sem.lsent)
+    tr = []
+    for i in range(3):
+        d = direct[i]
+        k = plan(T, topo, d)[0].index(rank)
+        tr.append(transfer(T.cores[d], eg_dir[i], sem.ld, T.l16[:, K * d:K * d + K], T.offd[:, K * k:K * k + K]))
+    g.remote_dma_fused(tr, local_sem=sem.lsent)
+    mine = slice(S * rank, S * rank + S)
+    sent = 0
+    g.wait_ge(sem.q1, 1)
+    tc, ts = [], []
+    for i in range(3):
+        d = direct[i]
+        c = slice(S * (1 + i), S * (2 + i))
+        tc.append(transfer(T.cores[d], eg_dir[i], sem["t%d" % rank], T.qc[:, c].bitcast(dt.uint8),
+                           T.wc[:, mine].bitcast(dt.uint8)))
+        ts.append(transfer(T.cores[d], eg_dir[i], sem["t%d" % rank], T.qs[:, c], T.ws[:, mine]))
+        sent += 2 * len(eg_dir[i])
+    g.remote_dma_fused(tc, local_sem=sem.tsent)
+    g.remote_dma_fused(ts, local_sem=sem.tsent)
+    for hf in range(2):
+        g.wait_ge(sem["q%d" % (2 + hf)], 1)
+        tc, ts = [], []
+        for j in range(2):
+            i = 2 * hf + j
+            c = slice(S * (4 + i), S * (5 + i))
+            eg = eg_half[hf][j]
+            tc.append(transfer(relays[i], eg, sem.rc, T.qc[:, c].bitcast(dt.uint8), T.rcode[:].bitcast(dt.uint8)))
+            ts.append(transfer(relays[i], eg, sem.rs, T.qs[:, c], T.rscal[:]))
+            sent += 2 * len(eg)
+        g.remote_dma_fused(tc, local_sem=sem.tsent)
+        g.remote_dma_fused(ts, local_sem=sem.tsent)
+    g.wait_ge(sem.tsent, sent)
+
+    need_d = 0
+    tile_need = {}
+    for d in direct:
+        e = [off[0:2], off[2:4], off[4:8]][plan(T, topo, d)[0].index(rank)]
+        need_d += len(e)
+        tile_need[d] = 2 * len(e)
+    need_o = [0, 0]
+    for i in range(4):
+        dd, dc, dr = plan(T, topo, cross[i])
+        n = len(topo.engines(dr[dc.index(rank)], core))
+        need_o[i // 2] += n
+        tile_need[cross[i]] = 2 * n
+
+    stages = [(0, 1, T.l16[:, K * rank:K * rank + K], None, 0),
+              (1, 4, T.offd[:], "ld", need_d),
+              (4, 6, T.offo[:, 0:2 * K], "lo0", need_o[0]),
+              (6, 8, T.offo[:, 2 * K:4 * K], "lo1", need_o[1])]
+    g.vector.wait_ge(sem.cwl, 16)
+    g.vector.tensor_copy(T.l16[:], T.lst[:]).then_inc(sem.conv, 1)
+    g.vector.wait_ge(sem.bkl, 16)
+    g.scalar.wait_ge(sem.bkl, 16)
+    for t in range(4):
+        out, in_ = T.win[:, S * t:S * t + S], T.book[:, t:4 * S:4]
+        if t < 2:
+            g.vector.tensor_copy(out, in_).then_inc(sem.vd, 1)
+        else:
+            g.scalar.activation(out, in_, copy).then_inc(sem.sd, 1)
+    g.vector.wait_ge(sem.vd, 2)
+    g.scalar.wait_ge(sem.sd, 2)
+    g.vector.wait_ge(sem.conv, 1)
+    g.scalar.wait_ge(sem.conv, 1)
+    for k, (lo, hi, offs, name, need) in enumerate(stages):
+        if name:
+            g.vector.wait_ge(sem[name], need)
+            g.scalar.wait_ge(sem[name], need)
+        for t in range(4):
+            out = T.h[:, 4 * S * lo + t:4 * S * hi:4]
+            src = T.win[:, S * t:S * t + S].indirect(offs)
+            if t < 2:
+                g.vector.tensor_copy(out, src).then_inc(sem["gv%d" % k], 1)
+            else:
+                g.scalar.activation(out, src, copy).then_inc(sem["gs%d" % k], 1)
+        g.vector.wait_ge(sem["gv%d" % k], 2)
+        g.vector.wait_ge(sem["gs%d" % k], 2)
+        g.vector.quantize_mx(T.qc[:, S * lo:S * hi], T.qs[:, S * lo:S * hi],
+                             T.h[:, 4 * S * lo:4 * S * hi]).then_inc(sem["q%d" % k], 1)
+    for i in range(2):
+        a, b = S * 4 * i, S * 4 * (i + 1)
+        g.vector.wait_ge(sem["x%d" % i], 16)
+        g.vector.quantize_mx(T.xc[:, a:b], T.xs[:, a:b], T.xt[:, 4 * a:4 * b]).then_inc(sem["qx%d" % i], 1)
+
+    order = [rank] + direct + cross
+    g.tensor.wait_ge(sem.q0, 1)
+    g.tensor.wait_ge(sem.qx0, 1)
+    g.tensor.wait_ge(sem.qx1, 1)
+    for n, s in enumerate(order):
+        c = slice(S * s, S * s + S)
+        if s == rank:
+            w, wsc = T.qc[:, 0:S], T.qs[:, 0:S]
+        else:
+            g.tensor.wait_ge(sem["t%d" % s], tile_need[s])
+            w, wsc = T.wc[:, c], T.ws[:, c]
+        mm = g.tensor.matmul_mx(T.ps[:, 0:S], T.xc[:, c], T.xs[:, c], w, wsc, n == 0, n == N - 1)
+        if n == N - 1:
+            mm.then_inc(sem.mm, 1)
+    g.vector.wait_ge(sem.mm, 1)
+    g.vector.tensor_copy(T.yt[:], T.ps[:, 0:S]).then_inc(sem.ev, 1)
+    g.sync.wait_ge(sem.ev, 1)
+    g.sync.dma_start(T.y[:], T.yt[:]).then_inc(sem.st, 16)
+    g.sync.wait_ge(sem.st, 16)
+
+
+def relay_program(g, core, T, topo):
+    owner = [c for c in topo.cores_of(core) if T.rank_of(c) is not None]
+    if not owner:
+        return
+    rank = T.rank_of(owner[0])
+    direct, cross, relays = plan(T, topo, rank)
+    if core not in relays:
+        return
+    sem = T.sem
+    i = relays.index(core)
+    to = T.cores[cross[i]]
+    rid, pid = topo.addr(to, core)
+    m = topo.mask(core, to)
+    n = len(topo.engines(core, to))
+    there = plan(T, topo, cross[i])[1].index(rank)
+    mine = slice(S * rank, S * rank + S)
+    g.wait_ge(sem.rl, 2)
+    g.remote_dma(T.offo[:, K * there:K * there + K], T.rlist[:], sem["lo%d" % (there // 2)], sem.rsent, pid, rid, m)
+    e = 4 if i < 2 else 8
+    g.wait_ge(sem.rc, e)
+    g.remote_dma(T.wc[:, mine].bitcast(dt.uint8), T.rcode[:].bitcast(dt.uint8), sem["t%d" % rank], sem.rsent, pid, rid, m)
+    g.wait_ge(sem.rs, e)
+    g.remote_dma(T.ws[:, mine], T.rscal[:], sem["t%d" % rank], sem.rsent, pid, rid, m)
+    g.wait_ge(sem.rsent, 3 * n)

@@ -2,6 +2,7 @@ from concourse.bass import DstId, RemoteDMATransfer
 from concourse.mybir import dt, ActivationFunctionType
 
 N = 8
+WORLD = 256
 S = 128
 K = S // 16
 SCRATCH = {
@@ -9,8 +10,7 @@ SCRATCH = {
     "l16": ("sbuf", [128, N * K], "uint16"),
     "book": ("sbuf", [128, 4 * S], "bfloat16"),
     "win": ("sbuf", [128, 4 * S], "bfloat16"),
-    "offd": ("sbuf", [128, 3 * K], "uint16"),
-    "offo": ("sbuf", [128, 4 * K], "uint16"),
+    "offs": ("sbuf", [128, N * K], "uint16"),
     "h": ("sbuf", [128, 4 * S * N], "bfloat16"),
     "qc": ("sbuf", [128, S * N], "float8_e4m3fn_x4"),
     "qs": ("sbuf", [128, S * N], "uint8"),
@@ -21,13 +21,35 @@ SCRATCH = {
     "ws": ("sbuf", [128, S * N], "uint8"),
     "ps": ("psum", [128, 512], "float32"),
     "yt": ("sbuf", [128, S], "float32"),
-    "rlist": ("sbuf", [128, K], "uint16"),
-    "rcode": ("sbuf", [128, S], "float8_e4m3fn_x4"),
-    "rscal": ("sbuf", [128, S], "uint8"),
+    "rlist": ("sbuf", [128, N * K], "uint16"),
+    "rcode": ("sbuf", [128, S * N], "float8_e4m3fn_x4"),
+    "rscal": ("sbuf", [128, S * N], "uint8"),
 }
-SEMAPHORES = (["cwl", "bkl", "x0", "x1", "conv", "vd", "sd", "lsent", "tsent", "ld", "lo0", "lo1", "qx0", "qx1", "mm", "ev",
-               "st", "rl", "rc", "rs", "rsent"]
-              + ["gv%d" % i for i in range(4)] + ["gs%d" % i for i in range(4)] + ["q%d" % i for i in range(4)]
+
+F0, N0, F1, N1, M0, M1 = range(6)
+LIST_STAGES = [(1, 2), (2, 4), (4, 6), (6, 8)]
+WORK = [("v", 0, 1, 0), ("v", 0, 1, 1), ("s", 0, 1, 2), ("s", 0, 1, 3), ("q", 0, 1), ("x", 0),
+        ("v", 2, 4, 0), ("v", 2, 4, 1), ("s", 2, 4, 2), ("s", 2, 4, 3), ("q", 2, 4),
+        ("s", 1, 2, 2), ("s", 1, 2, 3),
+        ("v", 4, 6, 0), ("v", 4, 6, 1), ("s", 4, 6, 2), ("s", 4, 6, 3), ("q", 4, 6),
+        ("v", 6, 8, 0), ("v", 6, 7, 1), ("s", 6, 8, 2), ("s", 6, 8, 3), ("s", 7, 8, 1), ("q", 6, 7), ("q", 7, 8),
+        ("v", 1, 2, 0), ("s", 1, 2, 1), ("q", 1, 2),
+        ("x", 1)]
+SENDS = [[("l", 4, 5, F0, "spare0"), ("l", 5, 6, N0, "spare1")],
+         [("l", 2, 3, None, "off0"), ("l", 3, 4, None, "off1"), ("l", 6, 7, F1, "spare")],
+         [("l", 7, 8, M0, "off")], [("l", 1, 2, None, "off")],
+         [("c", 2, 3, F0, "even"), ("c", 3, 4, N1, "odd")], [("s", 2, 4, N0, "all")],
+         [("c", 4, 5, M0, "off"), ("c", 5, 6, F0, "spare")], [("s", 4, 6, N0, "all")],
+         [("c", 6, 7, F1, "all")], [("c", 7, 7.5, N1, "spare"), ("c", 7.5, 8, M0, "off")],
+         [("s", 6, 7, F0, "even"), ("s", 7, 8, N0, "odd")],
+         [("c", 1, 2, None, "off")], [("s", 1, 2, None, "off")]]
+PRODUCTS = [0, 2, 3, 4, 5, 6, 1, 7]
+EARLY = 5
+X_SPLIT = 4
+
+SEMAPHORES = (["cwl", "bkl", "x0", "x1", "conv", "vd", "sd", "first", "sent", "qx0", "qx1", "mm", "ev", "st"]
+              + ["g%d" % i for i in range(N)] + ["q%d" % i for i in range(N)]
+              + ["l%d" % i for i in range(len(LIST_STAGES))] + ["r%d" % i for i in range(6)]
               + ["t%d" % i for i in range(N)])
 
 
@@ -38,19 +60,62 @@ def bits(engines):
     return m
 
 
-def plan(T, topo, rank):
+def peers(T, topo, rank):
     me = T.cores[rank]
-    direct = [r for r in range(N) if r != rank and topo.may_write(me, T.cores[r])]
-    cross = [r for r in range(N) if r != rank and r not in direct]
-    a = sorted(direct + [rank]).index(rank) % len(cross)
-    cross = cross[a:] + cross[:a]
-    cand = [c for c in topo.cores_of(me) if c != me and all(topo.may_write(c, T.cores[r]) for r in cross)]
+    side = [r for r in range(N) if r == rank or topo.may_write(me, T.cores[r])]
+    other = [r for r in range(N) if r not in side]
+    a = side.index(rank)
+    return [side[a ^ k] for k in range(len(side))] + [other[(k - a) % len(other)] for k in range(len(other))]
+
+
+def relays(T, topo, rank):
+    me, there = T.cores[rank], T.cores[peers(T, topo, rank)[-1]]
+    cand = [c for c in topo.cores_of(me) if topo.may_write(c, there)]
     near = [c for c in cand if topo.die(c) == topo.die(me)]
     far = [c for c in cand if topo.die(c) != topo.die(me)]
-    relays = []
-    for i in range(max(len(near), len(far))):
-        relays += far[i:i + 1] + near[i:i + 1]
-    return direct, cross, relays[:len(cross)]
+    mate = [c for c in range(WORLD) if topo.mates(c, me) and topo.may_write(c, me) and topo.die(c) == topo.die(me)]
+    return [far[0], near[0], far[1], near[1]] + mate
+
+
+def split(engines, n):
+    k = len(engines) // n
+    return [engines[i * k:i * k + k] for i in range(n)]
+
+
+def shares(T, topo, rank):
+    me = T.cores[rank]
+    off = topo.engines(me, T.cores[peers(T, topo, rank)[1]])
+    every = topo.engines(me, relays(T, topo, rank)[F0])
+    spare = [e for e in every if e not in off]
+    return {"off": off, "off0": split(off, 2)[0], "off1": split(off, 2)[1], "all": every, "even": every[0::2],
+            "odd": every[1::2], "spare": spare, "spare0": split(spare, 2)[0], "spare1": split(spare, 2)[1]}
+
+
+def jobs(i):
+    return [p for call in SENDS for p in call if p[3] == i]
+
+
+def parts(lo, hi):
+    return [(k, max(lo, k), min(hi, k + 1)) for k in range(N) if max(lo, k) < min(hi, k + 1)]
+
+
+def view(buffers, kind, lo, hi):
+    lists, codes, scales = buffers
+    if kind == "l":
+        return lists[:, K * lo:K * hi]
+    a, b = int(S * lo), int(S * hi)
+    return codes[:, a:b].bitcast(dt.uint8) if kind == "c" else scales[:, a:b]
+
+
+def arrival(kind, k):
+    if kind == "l":
+        return "l%d" % [n for n, (lo, hi) in enumerate(LIST_STAGES) if lo <= k < hi][0]
+    return "t%d" % k
+
+
+def transfer(topo, core, to, engines, rsem, src, dst):
+    rid, pid = topo.addr(to, core)
+    return RemoteDMATransfer(dst_ids=[DstId(rid=rid, pnc=pid)], dma_engine_mask=bits(engines), remote_sem=rsem, src=src, dst=dst)
 
 
 def rank_program(g, core, T, topo):
@@ -59,84 +124,47 @@ def rank_program(g, core, T, topo):
         relay_program(g, core, T, topo)
         return
     sem = T.sem
-    direct, cross, relays = plan(T, topo, rank)
+    peer = peers(T, topo, rank)
+    eng = shares(T, topo, rank)
     copy = ActivationFunctionType.Copy
-    off = topo.engines(core, T.cores[direct[0]])
-    spare = [e for e in topo.engines(core, relays[0]) if e not in off]
-
-    def transfer(to, engines, rsem, src, dst):
-        rid, pid = topo.addr(to, core)
-        return RemoteDMATransfer(dst_ids=[DstId(rid=rid, pnc=pid)], dma_engine_mask=bits(engines), remote_sem=rsem,
-                                 src=src, dst=dst)
-
-    eg_list = [spare[2 * i:2 * i + 2] for i in range(4)]
-    eg_dir = [off[0:2], off[2:4], off[4:8]]
-    eg_half = [[spare[0:4], spare[4:8]], [off[0:4] + spare[0:4], off[4:8] + spare[4:8]]]
+    steps = [w for w in WORK if w[0] == "q"]
+    q_at = {k: n for n, w in enumerate(steps) for k in range(w[1], w[2])}
 
     g.sync.dma_start(T.lst[:], T.cw[:]).then_inc(sem.cwl, 16)
     g.sync.dma_start(T.book[:], T.bk[:]).then_inc(sem.bkl, 16)
-    nlist = sum(len(e) for e in eg_list) + sum(len(e) for e in eg_dir)
-    g.sync.wait_ge(sem.lsent, nlist)
-    half = 2 * S * N
-    for i in range(2):
-        g.sync.dma_start(T.xt[:, i * half:(i + 1) * half], T.x[:, i * half:(i + 1) * half]).then_inc(sem["x%d" % i], 16)
+    cut = 4 * S * X_SPLIT
+    g.sync.dma_start(T.xt[:, 0:cut], T.x[:, 0:cut]).then_inc(sem.x0, 16)
+    g.sync.wait_ge(sem.first, sum(len(eng[p[4]]) for p in SENDS[0]))
+    g.sync.dma_start(T.xt[:, cut:4 * S * N], T.x[:, cut:4 * S * N]).then_inc(sem.x1, 16)
 
+    need, sent, ready = {}, 0, set()
     g.wait_ge(sem.conv, 1)
-    tr = []
-    for i in range(4):
-        d = cross[i]
-        tr.append(transfer(relays[i], eg_list[i], sem.rl, T.l16[:, K * d:K * d + K], T.rlist[:]))
-    g.remote_dma_fused(tr, local_sem=sem.lsent)
-    tr = []
-    for i in range(3):
-        d = direct[i]
-        k = plan(T, topo, d)[0].index(rank)
-        tr.append(transfer(T.cores[d], eg_dir[i], sem.ld, T.l16[:, K * d:K * d + K], T.offd[:, K * k:K * k + K]))
-    g.remote_dma_fused(tr, local_sem=sem.lsent)
-    mine = slice(S * rank, S * rank + S)
-    sent = 0
-    g.wait_ge(sem.q1, 1)
-    tc, ts = [], []
-    for i in range(3):
-        d = direct[i]
-        c = slice(S * (1 + i), S * (2 + i))
-        tc.append(transfer(T.cores[d], eg_dir[i], sem["t%d" % rank], T.qc[:, c].bitcast(dt.uint8),
-                           T.wc[:, mine].bitcast(dt.uint8)))
-        ts.append(transfer(T.cores[d], eg_dir[i], sem["t%d" % rank], T.qs[:, c], T.ws[:, mine]))
-        sent += 2 * len(eg_dir[i])
-    g.remote_dma_fused(tc, local_sem=sem.tsent)
-    g.remote_dma_fused(ts, local_sem=sem.tsent)
-    for hf in range(2):
-        g.wait_ge(sem["q%d" % (2 + hf)], 1)
-        tc, ts = [], []
-        for j in range(2):
-            i = 2 * hf + j
-            c = slice(S * (4 + i), S * (5 + i))
-            eg = eg_half[hf][j]
-            tc.append(transfer(relays[i], eg, sem.rc, T.qc[:, c].bitcast(dt.uint8), T.rcode[:].bitcast(dt.uint8)))
-            ts.append(transfer(relays[i], eg, sem.rs, T.qs[:, c], T.rscal[:]))
-            sent += 2 * len(eg)
-        g.remote_dma_fused(tc, local_sem=sem.tsent)
-        g.remote_dma_fused(ts, local_sem=sem.tsent)
-    g.wait_ge(sem.tsent, sent)
+    for n, call in enumerate(SENDS):
+        tr = []
+        for p in call:
+            kind, lo, hi, via, share = p
+            if kind == "l":
+                src = view((T.l16,) * 3, kind, peer[lo], peer[lo] + 1)
+            else:
+                src = view((None, T.qc, T.qs), kind, lo, hi)
+                for q in sorted({q_at[k] for k, a, b in parts(lo, hi)} - ready):
+                    g.wait_ge(sem["q%d" % q], 1)
+                    ready.add(q)
+            if via is None:
+                tr.append(transfer(topo, core, T.cores[peer[lo]], eng[share], sem[arrival(kind, lo)], src,
+                                   view((T.offs, T.wc, T.ws), kind, lo, hi)))
+                need[arrival(kind, lo)] = need.get(arrival(kind, lo), 0) + len(eng[share])
+            else:
+                to = relays(T, topo, rank if via < M0 else peer[int(lo)])[via]
+                tr.append(transfer(topo, core, to, eng[share], sem["r%d" % jobs(via).index(p)], src,
+                                   view((T.rlist, T.rcode, T.rscal), kind, lo, hi)))
+                for k, a, b in parts(lo, hi):
+                    need[arrival(kind, k)] = need.get(arrival(kind, k), 0) + len(eng["off"]) // len(parts(lo, hi))
+            if n:
+                sent += len(eng[share])
+        g.remote_dma_fused(tr, local_sem=sem.sent if n else sem.first)
+    g.wait_ge(sem.sent, sent)
 
-    need_d = 0
-    tile_need = {}
-    for d in direct:
-        e = [off[0:2], off[2:4], off[4:8]][plan(T, topo, d)[0].index(rank)]
-        need_d += len(e)
-        tile_need[d] = 2 * len(e)
-    need_o = [0, 0]
-    for i in range(4):
-        dd, dc, dr = plan(T, topo, cross[i])
-        n = len(topo.engines(dr[dc.index(rank)], core))
-        need_o[i // 2] += n
-        tile_need[cross[i]] = 2 * n
-
-    stages = [(0, 1, T.l16[:, K * rank:K * rank + K], None, 0),
-              (1, 4, T.offd[:], "ld", need_d),
-              (4, 6, T.offo[:, 0:2 * K], "lo0", need_o[0]),
-              (6, 8, T.offo[:, 2 * K:4 * K], "lo1", need_o[1])]
     g.vector.wait_ge(sem.cwl, 16)
     g.vector.tensor_copy(T.l16[:], T.lst[:]).then_inc(sem.conv, 1)
     g.vector.wait_ge(sem.bkl, 16)
@@ -147,43 +175,55 @@ def rank_program(g, core, T, topo):
             g.vector.tensor_copy(out, in_).then_inc(sem.vd, 1)
         else:
             g.scalar.activation(out, in_, copy).then_inc(sem.sd, 1)
-    g.vector.wait_ge(sem.vd, 2)
-    g.scalar.wait_ge(sem.sd, 2)
-    g.vector.wait_ge(sem.conv, 1)
-    g.scalar.wait_ge(sem.conv, 1)
-    for k, (lo, hi, offs, name, need) in enumerate(stages):
-        if name:
-            g.vector.wait_ge(sem[name], need)
-            g.scalar.wait_ge(sem[name], need)
-        for t in range(4):
+    for queue in (g.vector, g.scalar):
+        queue.wait_ge(sem.vd, 2)
+        queue.wait_ge(sem.sd, 2)
+        queue.wait_ge(sem.conv, 1)
+    count = [0] * len(steps)
+    seen = {"v": set(), "s": set()}
+    for w in WORK:
+        if w[0] in "vs":
+            count[q_at[w[1]]] += 1
+    for w in WORK:
+        if w[0] in "vs":
+            who, lo, hi, t = w
+            queue = g.vector if who == "v" else g.scalar
+            for name in sorted({arrival("l", k) for k in range(max(lo, 1), hi)} - seen[who]):
+                queue.wait_ge(sem[name], need[name])
+                seen[who].add(name)
+            offs = T.l16[:, K * rank:K * rank + K] if lo == 0 else T.offs[:, K * lo:K * hi]
             out = T.h[:, 4 * S * lo + t:4 * S * hi:4]
             src = T.win[:, S * t:S * t + S].indirect(offs)
-            if t < 2:
-                g.vector.tensor_copy(out, src).then_inc(sem["gv%d" % k], 1)
+            if who == "v":
+                g.vector.tensor_copy(out, src).then_inc(sem["g%d" % q_at[lo]], 1)
             else:
-                g.scalar.activation(out, src, copy).then_inc(sem["gs%d" % k], 1)
-        g.vector.wait_ge(sem["gv%d" % k], 2)
-        g.vector.wait_ge(sem["gs%d" % k], 2)
-        g.vector.quantize_mx(T.qc[:, S * lo:S * hi], T.qs[:, S * lo:S * hi],
-                             T.h[:, 4 * S * lo:4 * S * hi]).then_inc(sem["q%d" % k], 1)
-    for i in range(2):
-        a, b = S * 4 * i, S * 4 * (i + 1)
-        g.vector.wait_ge(sem["x%d" % i], 16)
-        g.vector.quantize_mx(T.xc[:, a:b], T.xs[:, a:b], T.xt[:, 4 * a:4 * b]).then_inc(sem["qx%d" % i], 1)
+                g.scalar.activation(out, src, copy).then_inc(sem["g%d" % q_at[lo]], 1)
+        elif w[0] == "q":
+            lo, hi = w[1], w[2]
+            g.vector.wait_ge(sem["g%d" % q_at[lo]], count[q_at[lo]])
+            g.vector.quantize_mx(T.qc[:, S * lo:S * hi], T.qs[:, S * lo:S * hi],
+                                 T.h[:, 4 * S * lo:4 * S * hi]).then_inc(sem["q%d" % q_at[lo]], 1)
+        else:
+            lo, hi = (0, X_SPLIT) if w[1] == 0 else (X_SPLIT, N)
+            g.vector.wait_ge(sem["x%d" % w[1]], 16)
+            g.vector.quantize_mx(T.xc[:, S * lo:S * hi], T.xs[:, S * lo:S * hi],
+                                 T.xt[:, 4 * S * lo:4 * S * hi]).then_inc(sem["qx%d" % w[1]], 1)
 
-    order = [rank] + direct + cross
-    g.tensor.wait_ge(sem.q0, 1)
+    g.tensor.wait_ge(sem["q%d" % q_at[0]], 1)
     g.tensor.wait_ge(sem.qx0, 1)
-    g.tensor.wait_ge(sem.qx1, 1)
-    for n, s in enumerate(order):
-        c = slice(S * s, S * s + S)
-        if s == rank:
+    first = [k for k in PRODUCTS[:EARLY] if peer[k] < X_SPLIT]
+    order = first + [k for k in PRODUCTS if k not in first]
+    for k in order:
+        if k == order[len(first)]:
+            g.tensor.wait_ge(sem.qx1, 1)
+        c = slice(S * peer[k], S * peer[k] + S)
+        if k == 0:
             w, wsc = T.qc[:, 0:S], T.qs[:, 0:S]
         else:
-            g.tensor.wait_ge(sem["t%d" % s], tile_need[s])
-            w, wsc = T.wc[:, c], T.ws[:, c]
-        mm = g.tensor.matmul_mx(T.ps[:, 0:S], T.xc[:, c], T.xs[:, c], w, wsc, n == 0, n == N - 1)
-        if n == N - 1:
+            g.tensor.wait_ge(sem["t%d" % k], need["t%d" % k])
+            w, wsc = T.wc[:, S * k:S * k + S], T.ws[:, S * k:S * k + S]
+        mm = g.tensor.matmul_mx(T.ps[:, 0:S], T.xc[:, c], T.xs[:, c], w, wsc, k == order[0], k == order[-1])
+        if k == order[-1]:
             mm.then_inc(sem.mm, 1)
     g.vector.wait_ge(sem.mm, 1)
     g.vector.tensor_copy(T.yt[:], T.ps[:, 0:S]).then_inc(sem.ev, 1)
@@ -193,26 +233,22 @@ def rank_program(g, core, T, topo):
 
 
 def relay_program(g, core, T, topo):
-    owner = [c for c in topo.cores_of(core) if T.rank_of(c) is not None]
-    if not owner:
+    role = [(r, relays(T, topo, r).index(core)) for r in range(N) if core in relays(T, topo, r)]
+    if not role or not jobs(role[0][1]):
         return
-    rank = T.rank_of(owner[0])
-    direct, cross, relays = plan(T, topo, rank)
-    if core not in relays:
-        return
+    rank, i = role[0]
     sem = T.sem
-    i = relays.index(core)
-    to = T.cores[cross[i]]
-    rid, pid = topo.addr(to, core)
-    m = topo.mask(core, to)
-    n = len(topo.engines(core, to))
-    there = plan(T, topo, cross[i])[1].index(rank)
-    mine = slice(S * rank, S * rank + S)
-    g.wait_ge(sem.rl, 2)
-    g.remote_dma(T.offo[:, K * there:K * there + K], T.rlist[:], sem["lo%d" % (there // 2)], sem.rsent, pid, rid, m)
-    e = 4 if i < 2 else 8
-    g.wait_ge(sem.rc, e)
-    g.remote_dma(T.wc[:, mine].bitcast(dt.uint8), T.rcode[:].bitcast(dt.uint8), sem["t%d" % rank], sem.rsent, pid, rid, m)
-    g.wait_ge(sem.rs, e)
-    g.remote_dma(T.ws[:, mine], T.rscal[:], sem["t%d" % rank], sem.rsent, pid, rid, m)
-    g.wait_ge(sem.rsent, 3 * n)
+    peer = peers(T, topo, rank)
+    eng = shares(T, topo, rank)
+    sent = 0
+    for n, (kind, lo, hi, via, share) in enumerate(jobs(i)):
+        g.wait_ge(sem["r%d" % n], len(eng[share]))
+        tr = []
+        for j, (k, a, b) in enumerate(parts(lo, hi)):
+            to = T.cores[peer[k] if i < M0 else rank]
+            e = split(topo.engines(core, to), len(parts(lo, hi)))[j]
+            tr.append(transfer(topo, core, to, e, sem[arrival(kind, k)], view((T.rlist, T.rcode, T.rscal), kind, a, b),
+                               view((T.offs, T.wc, T.ws), kind, a, b)))
+            sent += len(e)
+        g.remote_dma_fused(tr, local_sem=sem.sent)
+    g.wait_ge(sem.sent, sent)

from concourse.bass import DstId, RemoteDMATransfer
from concourse.mybir import dt, ActivationFunctionType

N = 8
WORLD = 256
S = 128
K = S // 16
SCRATCH = {
    "lst": ("sbuf", [128, N * K], "int32"),
    "l16": ("sbuf", [128, N * K], "uint16"),
    "book": ("sbuf", [128, 4 * S], "bfloat16"),
    "win": ("sbuf", [128, 4 * S], "bfloat16"),
    "offs": ("sbuf", [128, N * K], "uint16"),
    "h": ("sbuf", [128, 4 * S * N], "bfloat16"),
    "qc": ("sbuf", [128, S * N], "float8_e4m3fn_x4"),
    "qs": ("sbuf", [128, S * N], "uint8"),
    "xt": ("sbuf", [128, 4 * S * N], "bfloat16"),
    "xc": ("sbuf", [128, S * N], "float8_e4m3fn_x4"),
    "xs": ("sbuf", [128, S * N], "uint8"),
    "wc": ("sbuf", [128, S * N], "float8_e4m3fn_x4"),
    "ws": ("sbuf", [128, S * N], "uint8"),
    "ps": ("psum", [128, 512], "float32"),
    "yt": ("sbuf", [128, S], "float32"),
    "rlist": ("sbuf", [128, N * K], "uint16"),
    "rcode": ("sbuf", [128, S * N], "float8_e4m3fn_x4"),
    "rscal": ("sbuf", [128, S * N], "uint8"),
}

F0, N0, F1, N1, M0, M1 = range(6)
LIST_STAGES = [(1, 2), (2, 4), (4, 6), (6, 8)]
WORK = [("v", 0, 1, 0), ("v", 0, 1, 1), ("s", 0, 1, 2), ("s", 0, 1, 3), ("q", 0, 1), ("x", 0),
        ("v", 2, 4, 0), ("v", 2, 4, 1), ("s", 2, 4, 2), ("s", 2, 4, 3), ("q", 2, 4),
        ("s", 1, 2, 2), ("s", 1, 2, 3),
        ("v", 4, 6, 0), ("v", 4, 6, 1), ("s", 4, 6, 2), ("s", 4, 6, 3), ("q", 4, 6),
        ("v", 6, 8, 0), ("v", 6, 7, 1), ("s", 6, 8, 2), ("s", 6, 8, 3), ("s", 7, 8, 1), ("q", 6, 7), ("q", 7, 8),
        ("v", 1, 2, 0), ("s", 1, 2, 1), ("q", 1, 2),
        ("x", 1)]
SENDS = [[("l", 4, 5, F0, "spare0"), ("l", 5, 6, N0, "spare1")],
         [("l", 2, 3, None, "off0"), ("l", 3, 4, None, "off1"), ("l", 6, 7, F1, "spare")],
         [("l", 7, 8, M0, "off")], [("l", 1, 2, None, "off")],
         [("c", 2, 3, F0, "even"), ("c", 3, 4, N1, "odd")], [("s", 2, 4, N0, "all")],
         [("c", 4, 5, M0, "off"), ("c", 5, 6, F0, "spare")], [("s", 4, 6, N0, "all")],
         [("c", 6, 7, F1, "all")], [("c", 7, 7.5, N1, "spare"), ("c", 7.5, 8, M0, "off")],
         [("s", 6, 7, F0, "even"), ("s", 7, 8, N0, "odd")],
         [("c", 1, 2, None, "off")], [("s", 1, 2, None, "off")]]
PRODUCTS = [0, 2, 3, 4, 5, 6, 1, 7]
EARLY = 5
X_SPLIT = 4

SEMAPHORES = (["cwl", "bkl", "x0", "x1", "conv", "vd", "sd", "first", "sent", "qx0", "qx1", "mm", "ev", "st"]
              + ["g%d" % i for i in range(N)] + ["q%d" % i for i in range(N)]
              + ["l%d" % i for i in range(len(LIST_STAGES))] + ["r%d" % i for i in range(6)]
              + ["t%d" % i for i in range(N)])


def bits(engines):
    m = 0
    for e in engines:
        m |= 1 << e
    return m


def peers(T, topo, rank):
    me = T.cores[rank]
    side = [r for r in range(N) if r == rank or topo.may_write(me, T.cores[r])]
    other = [r for r in range(N) if r not in side]
    a = side.index(rank)
    return [side[a ^ k] for k in range(len(side))] + [other[(k - a) % len(other)] for k in range(len(other))]


def relays(T, topo, rank):
    me, there = T.cores[rank], T.cores[peers(T, topo, rank)[-1]]
    cand = [c for c in topo.cores_of(me) if topo.may_write(c, there)]
    near = [c for c in cand if topo.die(c) == topo.die(me)]
    far = [c for c in cand if topo.die(c) != topo.die(me)]
    mate = [c for c in range(WORLD) if topo.mates(c, me) and topo.may_write(c, me) and topo.die(c) == topo.die(me)]
    return [far[0], near[0], far[1], near[1]] + mate


def split(engines, n):
    k = len(engines) // n
    return [engines[i * k:i * k + k] for i in range(n)]


def shares(T, topo, rank):
    me = T.cores[rank]
    off = topo.engines(me, T.cores[peers(T, topo, rank)[1]])
    every = topo.engines(me, relays(T, topo, rank)[F0])
    spare = [e for e in every if e not in off]
    return {"off": off, "off0": split(off, 2)[0], "off1": split(off, 2)[1], "all": every, "even": every[0::2],
            "odd": every[1::2], "spare": spare, "spare0": split(spare, 2)[0], "spare1": split(spare, 2)[1]}


def jobs(i):
    return [p for call in SENDS for p in call if p[3] == i]


def parts(lo, hi):
    return [(k, max(lo, k), min(hi, k + 1)) for k in range(N) if max(lo, k) < min(hi, k + 1)]


def view(buffers, kind, lo, hi):
    lists, codes, scales = buffers
    if kind == "l":
        return lists[:, K * lo:K * hi]
    a, b = int(S * lo), int(S * hi)
    return codes[:, a:b].bitcast(dt.uint8) if kind == "c" else scales[:, a:b]


def arrival(kind, k):
    if kind == "l":
        return "l%d" % [n for n, (lo, hi) in enumerate(LIST_STAGES) if lo <= k < hi][0]
    return "t%d" % k


def transfer(topo, core, to, engines, rsem, src, dst):
    rid, pid = topo.addr(to, core)
    return RemoteDMATransfer(dst_ids=[DstId(rid=rid, pnc=pid)], dma_engine_mask=bits(engines), remote_sem=rsem, src=src, dst=dst)


def rank_program(g, core, T, topo):
    rank = T.rank_of(core)
    if rank is None:
        relay_program(g, core, T, topo)
        return
    sem = T.sem
    peer = peers(T, topo, rank)
    eng = shares(T, topo, rank)
    copy = ActivationFunctionType.Copy
    steps = [w for w in WORK if w[0] == "q"]
    q_at = {k: n for n, w in enumerate(steps) for k in range(w[1], w[2])}

    g.sync.dma_start(T.lst[:], T.cw[:]).then_inc(sem.cwl, 16)
    g.sync.dma_start(T.book[:], T.bk[:]).then_inc(sem.bkl, 16)
    cut = 4 * S * X_SPLIT
    g.sync.dma_start(T.xt[:, 0:cut], T.x[:, 0:cut]).then_inc(sem.x0, 16)
    g.sync.wait_ge(sem.first, sum(len(eng[p[4]]) for p in SENDS[0]))
    g.sync.dma_start(T.xt[:, cut:4 * S * N], T.x[:, cut:4 * S * N]).then_inc(sem.x1, 16)

    need, sent, ready = {}, 0, set()
    g.wait_ge(sem.conv, 1)
    for n, call in enumerate(SENDS):
        tr = []
        for p in call:
            kind, lo, hi, via, share = p
            if kind == "l":
                src = view((T.l16,) * 3, kind, peer[lo], peer[lo] + 1)
            else:
                src = view((None, T.qc, T.qs), kind, lo, hi)
                for q in sorted({q_at[k] for k, a, b in parts(lo, hi)} - ready):
                    g.wait_ge(sem["q%d" % q], 1)
                    ready.add(q)
            if via is None:
                tr.append(transfer(topo, core, T.cores[peer[lo]], eng[share], sem[arrival(kind, lo)], src,
                                   view((T.offs, T.wc, T.ws), kind, lo, hi)))
                need[arrival(kind, lo)] = need.get(arrival(kind, lo), 0) + len(eng[share])
            else:
                to = relays(T, topo, rank if via < M0 else peer[int(lo)])[via]
                tr.append(transfer(topo, core, to, eng[share], sem["r%d" % jobs(via).index(p)], src,
                                   view((T.rlist, T.rcode, T.rscal), kind, lo, hi)))
                for k, a, b in parts(lo, hi):
                    need[arrival(kind, k)] = need.get(arrival(kind, k), 0) + len(eng["off"]) // len(parts(lo, hi))
            if n:
                sent += len(eng[share])
        g.remote_dma_fused(tr, local_sem=sem.sent if n else sem.first)
    g.wait_ge(sem.sent, sent)

    g.vector.wait_ge(sem.cwl, 16)
    g.vector.tensor_copy(T.l16[:], T.lst[:]).then_inc(sem.conv, 1)
    g.vector.wait_ge(sem.bkl, 16)
    g.scalar.wait_ge(sem.bkl, 16)
    for t in range(4):
        out, in_ = T.win[:, S * t:S * t + S], T.book[:, t:4 * S:4]
        if t < 2:
            g.vector.tensor_copy(out, in_).then_inc(sem.vd, 1)
        else:
            g.scalar.activation(out, in_, copy).then_inc(sem.sd, 1)
    for queue in (g.vector, g.scalar):
        queue.wait_ge(sem.vd, 2)
        queue.wait_ge(sem.sd, 2)
        queue.wait_ge(sem.conv, 1)
    count = [0] * len(steps)
    seen = {"v": set(), "s": set()}
    for w in WORK:
        if w[0] in "vs":
            count[q_at[w[1]]] += 1
    for w in WORK:
        if w[0] in "vs":
            who, lo, hi, t = w
            queue = g.vector if who == "v" else g.scalar
            for name in sorted({arrival("l", k) for k in range(max(lo, 1), hi)} - seen[who]):
                queue.wait_ge(sem[name], need[name])
                seen[who].add(name)
            offs = T.l16[:, K * rank:K * rank + K] if lo == 0 else T.offs[:, K * lo:K * hi]
            out = T.h[:, 4 * S * lo + t:4 * S * hi:4]
            src = T.win[:, S * t:S * t + S].indirect(offs)
            if who == "v":
                g.vector.tensor_copy(out, src).then_inc(sem["g%d" % q_at[lo]], 1)
            else:
                g.scalar.activation(out, src, copy).then_inc(sem["g%d" % q_at[lo]], 1)
        elif w[0] == "q":
            lo, hi = w[1], w[2]
            g.vector.wait_ge(sem["g%d" % q_at[lo]], count[q_at[lo]])
            g.vector.quantize_mx(T.qc[:, S * lo:S * hi], T.qs[:, S * lo:S * hi],
                                 T.h[:, 4 * S * lo:4 * S * hi]).then_inc(sem["q%d" % q_at[lo]], 1)
        else:
            lo, hi = (0, X_SPLIT) if w[1] == 0 else (X_SPLIT, N)
            g.vector.wait_ge(sem["x%d" % w[1]], 16)
            g.vector.quantize_mx(T.xc[:, S * lo:S * hi], T.xs[:, S * lo:S * hi],
                                 T.xt[:, 4 * S * lo:4 * S * hi]).then_inc(sem["qx%d" % w[1]], 1)

    g.tensor.wait_ge(sem["q%d" % q_at[0]], 1)
    g.tensor.wait_ge(sem.qx0, 1)
    first = [k for k in PRODUCTS[:EARLY] if peer[k] < X_SPLIT]
    order = first + [k for k in PRODUCTS if k not in first]
    for k in order:
        if k == order[len(first)]:
            g.tensor.wait_ge(sem.qx1, 1)
        c = slice(S * peer[k], S * peer[k] + S)
        if k == 0:
            w, wsc = T.qc[:, 0:S], T.qs[:, 0:S]
        else:
            g.tensor.wait_ge(sem["t%d" % k], need["t%d" % k])
            w, wsc = T.wc[:, S * k:S * k + S], T.ws[:, S * k:S * k + S]
        mm = g.tensor.matmul_mx(T.ps[:, 0:S], T.xc[:, c], T.xs[:, c], w, wsc, k == order[0], k == order[-1])
        if k == order[-1]:
            mm.then_inc(sem.mm, 1)
    g.vector.wait_ge(sem.mm, 1)
    g.vector.tensor_copy(T.yt[:], T.ps[:, 0:S]).then_inc(sem.ev, 1)
    g.sync.wait_ge(sem.ev, 1)
    g.sync.dma_start(T.y[:], T.yt[:]).then_inc(sem.st, 16)
    g.sync.wait_ge(sem.st, 16)


def relay_program(g, core, T, topo):
    role = [(r, relays(T, topo, r).index(core)) for r in range(N) if core in relays(T, topo, r)]
    if not role or not jobs(role[0][1]):
        return
    rank, i = role[0]
    sem = T.sem
    peer = peers(T, topo, rank)
    eng = shares(T, topo, rank)
    sent = 0
    for n, (kind, lo, hi, via, share) in enumerate(jobs(i)):
        g.wait_ge(sem["r%d" % n], len(eng[share]))
        tr = []
        for j, (k, a, b) in enumerate(parts(lo, hi)):
            to = T.cores[peer[k] if i < M0 else rank]
            e = split(topo.engines(core, to), len(parts(lo, hi)))[j]
            tr.append(transfer(topo, core, to, e, sem[arrival(kind, k)], view((T.rlist, T.rcode, T.rscal), kind, a, b),
                               view((T.offs, T.wc, T.ws), kind, a, b)))
            sent += len(e)
        g.remote_dma_fused(tr, local_sem=sem.sent)
    g.wait_ge(sem.sent, sent)
